import numpy as np
import ml_dtypes


def mxq(x, axis, fmt="e4m3"):
    dtype, down = {"e4m3": (ml_dtypes.float8_e4m3fn, 7), "e5m2": (ml_dtypes.float8_e5m2, 14)}[fmt]
    v = np.moveaxis(np.asarray(x, np.float32).astype(ml_dtypes.bfloat16).astype(np.float64), axis, -1)
    blocks = v.reshape(v.shape[:-1] + (-1, 32))
    amax = np.abs(blocks).max(-1, keepdims=True)
    byte = np.maximum(np.where(amax > 0, np.frexp(amax)[1] - 1 + 127, 0) - down, 1)
    scale = np.exp2(byte - 127.0)
    codes = (blocks / scale).astype(np.float32).astype(dtype).astype(np.float64)
    return np.moveaxis((codes * scale).reshape(v.shape), -1, axis)


WIDE = False


def mx_kscale(k):
    if not WIDE:
        return np.ones(k)
    levels = np.array([10, -10, 5, -5, 0])
    if k % 512:
        return np.exp2(np.random.permutation(np.resize(levels, k // 32))).repeat(32)
    a = np.empty((k // 512, 16))
    for p in range(k // 512):
        a[p, :8] = np.random.permutation(np.resize(levels, 8))
        for g in range(8):
            far = levels[np.abs(levels - a[p, g]) >= 10]
            a[p, g + 8] = far[np.random.randint(len(far))]
    return np.exp2(a.ravel()).repeat(32)


def f64(x):
    return np.asarray(x).astype(np.float64)


def striped8(idx):
    return np.concatenate([x.reshape(-1, 16).T for x in idx]).astype(np.uint16)


def runs(offs, k):
    lists = np.stack([offs[16 * r : 16 * r + 16].T.reshape(-1) for r in range(8)]).astype(np.int64)
    return lists[np.arange(k) % 512 // 64]


def pack_weight(w):
    k, n = w.shape
    w = f64(np.asarray(w, np.float32).astype(ml_dtypes.bfloat16)).reshape(k // 32, 32, n)
    amax = np.abs(w).max(1)
    byte = np.clip(np.where(amax > 0, np.frexp(amax)[1] - 1 + 127 - 7, 1), 1, 254)
    scaled = (w * np.exp2(127.0 - byte)[:, None, :]).reshape(k, n).astype(np.float32)
    words = np.ascontiguousarray(scaled.reshape(k // 512, 128, 4, n).transpose(0, 1, 3, 2)).astype(ml_dtypes.float8_e4m3fn).view(np.uint8)
    return words, np.ascontiguousarray(byte.astype(np.uint8).reshape(k // 512, 16, n))


def unpack_weight(words, scales):
    g, p, n, _ = words.shape
    vals = np.ascontiguousarray(words).view(ml_dtypes.float8_e4m3fn).astype(np.float64) * np.repeat(np.exp2(scales.astype(np.float64) - 127.0), 8, axis=1)[..., None]
    return vals.transpose(0, 1, 3, 2).reshape(g * 512, n)


E2M1 = np.array([0.0, 0.5, 1.0, 1.5, 2.0, 3.0, 4.0, 6.0, -0.0, -0.5, -1.0, -1.5, -2.0, -3.0, -4.0, -6.0])


def pack_fp4(w):
    k, n = w.shape
    w = f64(np.asarray(w, np.float32).astype(ml_dtypes.bfloat16)).reshape(k // 32, 32, n)
    amax = np.abs(w).max(1)
    mant, ex = np.frexp(amax / 6.0)
    byte = np.clip(np.where(amax > 0, np.where(mant > 0.5, ex, ex - 1) + 127, 1), 1, 254)
    scaled = (w * np.exp2(127.0 - byte)[:, None, :]).reshape(k, n).astype(np.float32)
    c = np.ascontiguousarray(scaled.reshape(k // 512, 128, 4, n).transpose(0, 1, 3, 2)).astype(ml_dtypes.float4_e2m1fn).view(np.uint8) & 0xF
    words = (c[..., 0::2] | (c[..., 1::2] << 4)).reshape(k // 512, 128, 2 * n)
    return np.ascontiguousarray(words), np.ascontiguousarray(byte.astype(np.uint8).reshape(k // 512, 16, n))


def unpack_fp4(words, scales):
    g, _, n = scales.shape
    words = np.ascontiguousarray(words).reshape(g, 128, n, 2)
    nib = np.empty((g, 128, n, 4), np.uint8)
    nib[..., 0::2] = words & 0xF
    nib[..., 1::2] = words >> 4
    vals = E2M1[nib] * np.repeat(np.exp2(scales.astype(np.float64) - 127.0), 8, axis=1)[..., None]
    return vals.transpose(0, 1, 3, 2).reshape(g * 512, n)


def planes(y):
    n, m = y.shape
    v = y.astype(np.float32).astype(ml_dtypes.bfloat16).astype(np.float64).reshape(n // 32, 32, m)
    top = np.abs(v).max(1)
    byte = np.clip(np.where(top > 0, np.frexp(top)[1] - 1 + 127 - 7, 1), 1, 254)
    codes = (v * np.exp2(127.0 - byte)[:, None, :]).reshape(n, m).astype(np.float32).astype(ml_dtypes.float8_e4m3fn).view(np.uint8)
    words = codes.reshape(n // 512, 128, 4, m).transpose(0, 1, 3, 2)
    return np.ascontiguousarray(words), np.ascontiguousarray(byte.astype(np.uint8).reshape(n // 512, 16, m))


K, T, S, N, H, W = 512, 2048, 512, 512, 512, 256


def setup_inputs():
    n = np.random.standard_normal
    s = mx_kscale(K)[:, None]
    u = mx_kscale(H)
    packed_xT = pack_weight(n((K, T)) * s)
    packed_w1 = pack_fp4(n((K, H)) / np.sqrt(K) / s)
    packed_w2 = pack_fp4(n((H, N)) / np.sqrt(H) / u[:, None])
    perm = np.stack([np.random.permutation(S) for _ in range(8)])
    return {
        "x_words": packed_xT[0],
        "x_scales": packed_xT[1],
        "w1_words": packed_w1[0],
        "w1_scales": packed_w1[1],
        "gn": (np.random.uniform(0.5, 1.5, (H, 1)) * u[:, None]).astype(np.float32),
        "w2_words": packed_w2[0],
        "w2_scales": packed_w2[1],
        "offs": striped8(np.random.randint(0, T, (8, S))),
        "n1": striped8(perm[:, :W]),
        "n2": striped8(perm[:, W:]),
        "n3": striped8(np.stack([np.random.permutation(S) for _ in range(8)])),
        "n4": striped8(np.stack([np.random.permutation(S) for _ in range(8)])),
    }


def reference(x_words, x_scales, w1_words, w1_scales, gn, w2_words, w2_scales, offs, n1, n2, n3, n4):
    xq = unpack_weight(x_words, x_scales)[np.arange(K)[:, None], runs(offs, K)]
    y = unpack_fp4(w1_words, w1_scales).T @ xq
    pa = y[np.arange(H)[:, None], runs(n1, H)]
    pb = y[np.arange(H)[:, None], runs(n2, H)]
    rb = pa * pb
    ra = pa + pb
    ds = np.zeros((H, S))
    ds[np.arange(H)[:, None], runs(n1, H)] = ra
    dt = ds.copy()
    dt[np.arange(H)[:, None], runs(n2, H)] = rb
    z = f64(gn) * dt
    h = unpack_fp4(w2_words, w2_scales).T @ mxq(z, 0, "e4m3")
    out_0 = 0.75 * ((h - (h[np.arange(N)[:, None], runs(n3, N)])) * (h - (h[np.arange(N)[:, None], runs(n4, N)])))
    return (out_0,) + planes(out_0)

@@ -1,0 +1,255 @@
+from contextlib import ExitStack
+
+import concourse.mybir as mybir
+
+K, T, S, N, H, W = 512, 2048, 512, 512, 512, 256
+FLOPS = 2 * K * H * S + 2 * H * N * S
+
+F32 = mybir.dt.float32
+BF16 = mybir.dt.bfloat16
+I32 = mybir.dt.int32
+U32 = mybir.dt.uint32
+U16 = mybir.dt.uint16
+U8 = mybir.dt.uint8
+FP8X4 = mybir.dt.float8_e4m3fn_x4
+FP4X4 = mybir.dt.float4_e2m1fn_x4
+ALU = mybir.AluOpType
+COPY = mybir.ActivationFunctionType.Copy
+
+P = 128
+PACK = 4
+HALF = S // 2
+PER_COL = 16
+
+
+def tile_picked_hashbondquad_none_po_kernel(
+    tc, x_words, x_scales, w1_words, w1_scales, gn, w2_words, w2_scales, offs, n1, n2, n3, n4, out_0, out_1, out_2
+):
+    nc = tc.nc
+    with ExitStack() as ctx:
+        keep = ctx.enter_context(tc.tile_pool(name="keep", bufs=1))
+        psum = ctx.enter_context(tc.psum_pool(name="psum", bufs=8))
+
+        def sb(name, shape, dtype, tag=None):
+            return keep.tile(shape, dtype, name=name, tag=tag or name, align_bytes=64)
+
+        def entries(lst, c0, c1):
+            return lst[:, c0 // PER_COL : c1 // PER_COL]
+
+        offs_t = keep.tile([P, S // PER_COL], U16, name="offs_t")
+        n1_t = keep.tile([P, W // PER_COL], U16, name="n1_t")
+        n2_t = keep.tile([P, W // PER_COL], U16, name="n2_t")
+        n3_t = keep.tile([P, S // PER_COL], U16, name="n3_t")
+        n4_t = keep.tile([P, S // PER_COL], U16, name="n4_t")
+
+        xw = sb("xw", [P, T], I32)
+        xs = sb("xs", [P, T], U8)
+        w1w_raw = sb("w1w_raw", [P, 2 * H], U8)
+        w2w_raw = sb("w2w_raw", [P, 2 * N], U8)
+        ws_raw = sb("ws_raw", [P, H], U8)
+        xs_placed = sb("xs_placed", [P, S], U8)
+        gain = sb("gain", [P, PACK], F32)
+
+        nc.vector.memset(xs[:].bitcast(I32), 0)
+        nc.gpsimd.memset(ws_raw[:].bitcast(I32), 0)
+        nc.vector.memset(xs_placed[:].bitcast(I32), 0)
+
+        def load_scale_rows(queue, scales, q):
+            queue.dma_start(
+                out=ws_raw[32 * q : 32 * q + 4, :].bitcast(I32), in_=scales[0][4 * q : 4 * q + 4, :].bitcast(I32)
+            )
+
+        nc.sync.dma_start(offs_t[:], offs)
+        nc.sync.dma_start(out=xs[0:P:8, :].bitcast(I32), in_=x_scales[0].bitcast(I32))
+        nc.scalar.dma_start(out=w1w_raw[:].bitcast(I32), in_=w1_words[0].bitcast(I32))
+        nc.scalar.dma_start(out=xw[:], in_=x_words[0].rearrange("p n t -> p (n t)").bitcast(I32))
+        nc.sync.dma_start(n1_t[:], n1)
+        nc.sync.dma_start(n2_t[:], n2)
+        nc.sync.dma_start(n3_t[:], n3)
+        nc.sync.dma_start(n4_t[:], n4)
+        for q in range(4):
+            load_scale_rows(nc.gpsimd if q < 2 else nc.sync, w1_scales, q)
+        nc.gpsimd.dma_start(out=w2w_raw[:].bitcast(I32), in_=w2_words[0].bitcast(I32))
+        nc.gpsimd.dma_start(out=gain[:], in_=gn.rearrange("(p t) o -> p (t o)", t=PACK))
+
+        def deal_words(name, raw, tag):
+            dealt = sb(name, [P, 2 * H], U8, tag)
+            nc.vector.tensor_copy(
+                out=dealt[:].rearrange("p (t m b) -> p t m b", t=PACK, b=2),
+                in_=raw[:].rearrange("p (m t b) -> p t m b", t=PACK, b=2),
+            )
+            return dealt
+
+        def deal_scales(name, raw, tag):
+            dealt = sb(name, [P, H], U8, tag)
+            nc.vector.tensor_copy(
+                out=dealt[:].rearrange("p (t m) -> p t m", t=PACK),
+                in_=raw[:].rearrange("p (m t) -> p t m", t=PACK),
+            )
+            return dealt
+
+        def product(ww, ws, t, words, scales, c0, c1):
+            acc = psum.tile([P, c1 - c0], F32, name="acc")
+            nc.tensor.matmul_mx(
+                out=acc[:],
+                lhsT=ww[:, 2 * P * t : 2 * P * (t + 1)].bitcast(FP4X4),
+                lhsT_scale=ws[:, P * t : P * (t + 1)],
+                rhs=words[:, c0:c1].bitcast(FP8X4),
+                rhs_scale=scales[:, c0:c1],
+                start=True,
+                stop=True,
+            )
+            return acc
+
+        xs_picked = sb("xs_picked", [P, S], U8)
+        nc.vector.tensor_copy(out=xs_picked[:], in_=xs[:].indirect(offs_t[:]))
+        for q in range(4):
+            nc.scalar.dma_start(
+                out=xs_placed[32 * q : 32 * q + 4, :].bitcast(I32),
+                in_=xs_picked[32 * q : 32 * q + 32 : 8, :].bitcast(I32),
+            )
+        w1w = deal_words("w1w", w1w_raw, "xs")
+        xw_picked = sb("xw_picked", [P, S], U32, "w1w_raw")
+        for c0 in (0, HALF):
+            nc.vector.tensor_copy(
+                out=xw_picked[:, c0 : c0 + HALF], in_=xw[:].bitcast(U32).indirect(entries(offs_t, c0, c0 + HALF))
+            )
+        w1s = deal_scales("w1s", ws_raw, "xw")
+        for q in range(4):
+            load_scale_rows(nc.sync, w2_scales, q)
+        w2w = deal_words("w2w", w2w_raw, "xs_picked")
+        w2s = deal_scales("w2s", ws_raw, "w2s")
+
+        y = [sb(f"y{t}", [P, S], F32) for t in range(PACK)]
+        for t in range(PACK):
+            for c0, c1 in ((0, HALF), (HALF, S)) if t == 0 else ((0, S),):
+                acc = product(w1w, w1s, t, xw_picked, xs_placed, c0, c1)
+                nc.scalar.copy(out=y[t][:, c0:c1], in_=acc[:])
+
+        pa = [sb(f"pa{t}", [P, W], F32) for t in range(PACK)]
+        pb = [sb(f"pb{t}", [P, W], F32) for t in range(PACK)]
+        dt = [sb(f"dt{t}", [P, S], F32) for t in range(PACK)]
+        zb = [sb(f"zb{h}", [P, HALF, PACK], BF16) for h in range(2)]
+
+        def fetch_a(t):
+            nc.vector.tensor_copy(out=pa[t][:], in_=y[t][:].indirect(n1_t[:]))
+
+        def fetch_b(t):
+            nc.vector.tensor_copy(out=pb[t][:], in_=y[t][:].indirect(n2_t[:]))
+
+        def put_sum(t):
+            nc.vector.tensor_tensor(dt[t][:].indirect(n1_t[:]), pa[t][:], pb[t][:], ALU.add)
+
+        def put_product(t):
+            nc.vector.tensor_tensor(dt[t][:].indirect(n2_t[:]), pa[t][:], pb[t][:], ALU.mult)
+
+        def round_z_scalar(t, h):
+            nc.scalar.activation(
+                out=zb[h][:, :, t], in_=dt[t][:, h * HALF : (h + 1) * HALF], func=COPY, scale=gain[:, t : t + 1]
+            )
+
+        def round_z_vector(t, h):
+            nc.vector.tensor_scalar(
+                out=zb[h][:, :, t],
+                in0=dt[t][:, h * HALF : (h + 1) * HALF],
+                scalar1=gain[:, t : t + 1],
+                scalar2=None,
+                op0=ALU.mult,
+            )
+
+        fetch_a(0)
+        fetch_b(0)
+        for t in range(PACK):
+            last = t == PACK - 1
+            if not last:
+                fetch_a(t + 1)
+            put_sum(t)
+            if not last:
+                fetch_b(t + 1)
+            else:
+                round_z_vector(t - 1, 0)
+            put_product(t)
+            if t < 2:
+                round_z_scalar(t, 0)
+            round_z_scalar(t, 1)
+        round_z_vector(PACK - 1, 0)
+
+        zw = sb("zw", [P, S], U32)
+        zs = sb("zs", [P, S], U8)
+        for h in range(2):
+            cols = slice(h * HALF, (h + 1) * HALF)
+            nc.vector.quantize_mx(
+                out=zw[:, cols].bitcast(FP8X4), scales=zs[:, cols], in_=zb[h][:].rearrange("p c t -> p (c t)")
+            )
+
+        hw = [sb(f"hw{t}", [P, S], F32) for t in range(PACK)]
+        hp = [sb(f"hp{t}", [P, S], F32) for t in range(PACK)]
+        for t in range(PACK):
+            for c0, c1 in ((0, HALF), (HALF, S)) if t == 0 else ((0, S),):
+                acc = product(w2w, w2s, t, zw, zs, c0, c1)
+                nc.scalar.copy(out=hw[t][:, c0:c1], in_=acc[:])
+                nc.scalar.copy(out=hp[t][:, c0:c1], in_=acc[:])
+
+        d3 = sb("d3", [P, PACK, S], F32)
+        d4 = sb("d4", [P, PACK, S], F32)
+        res = sb("res", [P, PACK, S], F32)
+        resb = sb("resb", [P, S, PACK], BF16)
+        ow = sb("ow", [P, S], U32)
+        osc = sb("osc", [P, S], U8)
+        out_rows = out_0.rearrange("(p t) c -> p t c", t=PACK)
+        out_words = out_1[0].rearrange("p c t -> p (c t)").bitcast(I32)
+
+        def diff(dst, lst, t, c0, c1):
+            nc.vector.tensor_tensor(
+                dst[:, t, c0:c1], hw[t][:].indirect(entries(lst, c0, c1)), hp[t][:, c0:c1], ALU.subtract
+            )
+
+        def finish(t, c0, c1):
+            nc.vector.scalar_tensor_tensor(
+                out=res[:, t, c0:c1], in0=d3[:, t, c0:c1], scalar=0.75, in1=d4[:, t, c0:c1], op0=ALU.mult, op1=ALU.mult
+            )
+            nc.sync.dma_start(out=out_rows[:, t, c0:c1], in_=res[:, t, c0:c1])
+
+        def round_out(copy, t0, c0, c1):
+            copy(out=resb[:, c0:c1, t0 : t0 + 2], in_=res[:, t0 : t0 + 2, c0:c1].rearrange("p t c -> p c t"))
+
+        def quantise_out(c0, c1):
+            nc.vector.quantize_mx(
+                out=ow[:, c0:c1].bitcast(FP8X4),
+                scales=osc[:, c0:c1],
+                in_=resb[:, c0:c1, :].rearrange("p c t -> p (c t)"),
+            )
+            nc.sync.dma_start(out=out_words[:, c0:c1], in_=ow[:, c0:c1].bitcast(I32))
+
+        for t in range(PACK - 1):
+            diff(d3, n3_t, t, 0, HALF)
+            if t > 0:
+                finish(t - 1, 0, S)
+            if t == 2:
+                round_out(nc.scalar.copy, 0, 0, S)
+            diff(d4, n4_t, t, 0, HALF)
+            diff(d3, n3_t, t, HALF, S)
+            diff(d4, n4_t, t, HALF, S)
+        t = PACK - 1
+        a, b = HALF, HALF + HALF // 2
+        diff(d3, n3_t, t, 0, a)
+        finish(t - 1, 0, S)
+        diff(d4, n4_t, t, 0, a)
+        diff(d3, n3_t, t, a, b)
+        finish(t, 0, a)
+        round_out(nc.scalar.copy, 2, 0, a)
+        diff(d4, n4_t, t, a, b)
+        diff(d3, n3_t, t, b, S)
+        finish(t, a, b)
+        round_out(nc.scalar.copy, 2, a, b)
+        diff(d4, n4_t, t, b, S)
+        quantise_out(0, a)
+        finish(t, b, S)
+        quantise_out(a, b)
+        round_out(nc.vector.tensor_copy, 2, b, S)
+        quantise_out(b, S)
+        for q in range(4):
+            queue = nc.scalar if q % 2 == 0 else nc.sync
+            queue.dma_start(
+                out=out_2[0][4 * q : 4 * q + 4, :].bitcast(I32), in_=osc[32 * q : 32 * q + 4, :].bitcast(I32)
+            )

@@ -44,14 +44,12 @@ def tile_picked_hashbondquad_none_po_kernel(
 
         xw = sb("xw", [P, T], I32)
         xs = sb("xs", [P, T], U8)
-        w1w_raw = sb("w1w_raw", [P, 2 * H], U8)
-        w2w_raw = sb("w2w_raw", [P, 2 * N], U8)
+        ww_raw = sb("ww_raw", [P, 2 * H], U8)
         ws_raw = sb("ws_raw", [P, H], U8)
         xs_placed = sb("xs_placed", [P, S], U8)
-        gain = sb("gain", [P, PACK], F32)
 
-        nc.vector.memset(xs[:].bitcast(I32), 0)
-        nc.gpsimd.memset(ws_raw[:].bitcast(I32), 0)
+        nc.gpsimd.memset(xs[:].bitcast(I32), 0)
+        nc.vector.memset(ws_raw[:].bitcast(I32), 0)
         nc.vector.memset(xs_placed[:].bitcast(I32), 0)
 
         def load_scale_rows(queue, scales, q):
@@ -61,39 +59,36 @@ def tile_picked_hashbondquad_none_po_kernel(
 
         nc.sync.dma_start(offs_t[:], offs)
         nc.sync.dma_start(out=xs[0:P:8, :].bitcast(I32), in_=x_scales[0].bitcast(I32))
-        nc.scalar.dma_start(out=w1w_raw[:].bitcast(I32), in_=w1_words[0].bitcast(I32))
-        nc.scalar.dma_start(out=xw[:], in_=x_words[0].rearrange("p n t -> p (n t)").bitcast(I32))
         nc.sync.dma_start(n1_t[:], n1)
+        nc.sync.dma_start(out=xw[:], in_=x_words[0].rearrange("p n t -> p (n t)").bitcast(I32))
         nc.sync.dma_start(n2_t[:], n2)
         nc.sync.dma_start(n3_t[:], n3)
         nc.sync.dma_start(n4_t[:], n4)
+        nc.scalar.dma_start(out=ww_raw[:].bitcast(I32), in_=w1_words[0].bitcast(I32))
         for q in range(4):
-            load_scale_rows(nc.gpsimd if q < 2 else nc.sync, w1_scales, q)
-        nc.gpsimd.dma_start(out=w2w_raw[:].bitcast(I32), in_=w2_words[0].bitcast(I32))
-        nc.gpsimd.dma_start(out=gain[:], in_=gn.rearrange("(p t) o -> p (t o)", t=PACK))
+            load_scale_rows(nc.scalar if q < 2 else nc.gpsimd, w1_scales, q)
 
-        def deal_words(name, raw, tag):
-            dealt = sb(name, [P, 2 * H], U8, tag)
+        def deal_words(name, t0, t1, tag=None):
+            dealt = sb(name, [P, t1 - t0, 2 * P], U8, tag)
             nc.vector.tensor_copy(
-                out=dealt[:].rearrange("p (t m b) -> p t m b", t=PACK, b=2),
-                in_=raw[:].rearrange("p (m t b) -> p t m b", t=PACK, b=2),
+                out=dealt[:].rearrange("p t (m b) -> p t m b", b=2),
+                in_=ww_raw[:].rearrange("p (m t b) -> p t m b", t=PACK, b=2)[:, t0:t1],
             )
-            return dealt
+            return [dealt[:, t, :] for t in range(t1 - t0)]
 
-        def deal_scales(name, raw, tag):
-            dealt = sb(name, [P, H], U8, tag)
+        def deal_scales(name, t0, t1, tag=None):
+            dealt = sb(name, [P, t1 - t0, P], U8, tag)
             nc.vector.tensor_copy(
-                out=dealt[:].rearrange("p (t m) -> p t m", t=PACK),
-                in_=raw[:].rearrange("p (m t) -> p t m", t=PACK),
+                out=dealt[:], in_=ws_raw[:].rearrange("p (m t) -> p t m", t=PACK)[:, t0:t1]
             )
-            return dealt
+            return [dealt[:, t, :] for t in range(t1 - t0)]
 
         def product(ww, ws, t, words, scales, c0, c1):
             acc = psum.tile([P, c1 - c0], F32, name="acc")
             nc.tensor.matmul_mx(
                 out=acc[:],
-                lhsT=ww[:, 2 * P * t : 2 * P * (t + 1)].bitcast(FP4X4),
-                lhsT_scale=ws[:, P * t : P * (t + 1)],
+                lhsT=ww[t].bitcast(FP4X4),
+                lhsT_scale=ws[t],
                 rhs=words[:, c0:c1].bitcast(FP8X4),
                 rhs_scale=scales[:, c0:c1],
                 start=True,
@@ -104,21 +99,22 @@ def tile_picked_hashbondquad_none_po_kernel(
         xs_picked = sb("xs_picked", [P, S], U8)
         nc.vector.tensor_copy(out=xs_picked[:], in_=xs[:].indirect(offs_t[:]))
         for q in range(4):
-            nc.scalar.dma_start(
+            queue = nc.scalar if q % 2 == 0 else nc.sync
+            queue.dma_start(
                 out=xs_placed[32 * q : 32 * q + 4, :].bitcast(I32),
                 in_=xs_picked[32 * q : 32 * q + 32 : 8, :].bitcast(I32),
             )
-        w1w = deal_words("w1w", w1w_raw, "xs")
-        xw_picked = sb("xw_picked", [P, S], U32, "w1w_raw")
+        w1w = deal_words("w1w", 0, PACK, "xs")
+        nc.sync.dma_start(out=ww_raw[:].bitcast(I32), in_=w2_words[0].bitcast(I32))
+        xw_picked = sb("xw_picked", [P, S], U32)
         for c0 in (0, HALF):
             nc.vector.tensor_copy(
                 out=xw_picked[:, c0 : c0 + HALF], in_=xw[:].bitcast(U32).indirect(entries(offs_t, c0, c0 + HALF))
             )
-        w1s = deal_scales("w1s", ws_raw, "xw")
+        w1s = deal_scales("w1s", 0, PACK, "xw")
         for q in range(4):
             load_scale_rows(nc.sync, w2_scales, q)
-        w2w = deal_words("w2w", w2w_raw, "xs_picked")
-        w2s = deal_scales("w2s", ws_raw, "w2s")
+        w2w = deal_words("w2w_first", 0, 2, "xs_picked")
 
         y = [sb(f"y{t}", [P, S], F32) for t in range(PACK)]
         for t in range(PACK):
@@ -126,6 +122,8 @@ def tile_picked_hashbondquad_none_po_kernel(
                 acc = product(w1w, w1s, t, xw_picked, xs_placed, c0, c1)
                 nc.scalar.copy(out=y[t][:, c0:c1], in_=acc[:])
 
+        gain = sb("gain", [P, PACK], F32, "xw_picked")
+        nc.sync.dma_start(out=gain[:], in_=gn.rearrange("(p t) o -> p (t o)", t=PACK))
         pa = [sb(f"pa{t}", [P, W], F32) for t in range(PACK)]
         pb = [sb(f"pb{t}", [P, W], F32) for t in range(PACK)]
         dt = [sb(f"dt{t}", [P, S], F32) for t in range(PACK)]
@@ -169,6 +167,8 @@ def tile_picked_hashbondquad_none_po_kernel(
             else:
                 round_z_vector(t - 1, 0)
             put_product(t)
+            if t == 0:
+                w2s = deal_scales("w2s_first", 0, 2, "y1")
             if t < 2:
                 round_z_scalar(t, 0)
             round_z_scalar(t, 1)
@@ -182,13 +182,19 @@ def tile_picked_hashbondquad_none_po_kernel(
                 out=zw[:, cols].bitcast(FP8X4), scales=zs[:, cols], in_=zb[h][:].rearrange("p c t -> p (c t)")
             )
 
-        hw = [sb(f"hw{t}", [P, S], F32) for t in range(PACK)]
+        hw = [sb(f"hw{t}", [P, 2 * S if t in (1, 2) else S], F32) for t in range(PACK)]
         hp = [sb(f"hp{t}", [P, S], F32) for t in range(PACK)]
-        for t in range(PACK):
-            for c0, c1 in ((0, HALF), (HALF, S)) if t == 0 else ((0, S),):
-                acc = product(w2w, w2s, t, zw, zs, c0, c1)
-                nc.scalar.copy(out=hw[t][:, c0:c1], in_=acc[:])
-                nc.scalar.copy(out=hp[t][:, c0:c1], in_=acc[:])
+        first = [product(w2w, w2s, 0, zw, zs, h * HALF, (h + 1) * HALF) for h in range(2)]
+        w2w = w2w + deal_words("w2w_rest", 2, PACK, "zb1")
+        w2s = w2s + deal_scales("w2s_rest", 2, PACK, "zb0")
+        nc.scalar.copy(out=hw[0][:, :HALF], in_=first[0][:])
+        nc.scalar.copy(out=hw[0][:, HALF:], in_=first[1][:])
+        nc.vector.tensor_copy(out=hp[0][:, :HALF], in_=first[0][:])
+        nc.scalar.copy(out=hp[0][:, HALF:], in_=first[1][:])
+        for t in range(1, PACK):
+            acc = product(w2w, w2s, t, zw, zs, 0, S)
+            nc.scalar.copy(out=hw[t][:, :S], in_=acc[:])
+            nc.scalar.copy(out=hp[t][:], in_=acc[:])
 
         d3 = sb("d3", [P, PACK, S], F32)
         d4 = sb("d4", [P, PACK, S], F32)
@@ -221,15 +227,15 @@ def tile_picked_hashbondquad_none_po_kernel(
             )
             nc.sync.dma_start(out=out_words[:, c0:c1], in_=ow[:, c0:c1].bitcast(I32))
 
-        for t in range(PACK - 1):
-            diff(d3, n3_t, t, 0, HALF)
-            if t > 0:
-                finish(t - 1, 0, S)
-            if t == 2:
-                round_out(nc.scalar.copy, 0, 0, S)
-            diff(d4, n4_t, t, 0, HALF)
-            diff(d3, n3_t, t, HALF, S)
-            diff(d4, n4_t, t, HALF, S)
+        diff(d3, n3_t, 0, 0, HALF)
+        diff(d4, n4_t, 0, 0, HALF)
+        diff(d3, n3_t, 0, HALF, S)
+        diff(d4, n4_t, 0, HALF, S)
+        for t in (1, 2):
+            diff(d3, n3_t, t, 0, S)
+            finish(t - 1, 0, S)
+            diff(d4, n4_t, t, 0, S)
+        round_out(nc.scalar.copy, 0, 0, S)
         t = PACK - 1
         a, b = HALF, HALF + HALF // 2
         diff(d3, n3_t, t, 0, a)

@@ -18,8 +18,11 @@ COPY = mybir.ActivationFunctionType.Copy
 
 P = 128
 PACK = 4
+QUADS = 4
 HALF = S // 2
+LAST = S - S // 4
 PER_COL = 16
+PSUM_BANKS = 8
 
 
 def tile_picked_hashbondquad_none_po_kernel(
@@ -28,7 +31,7 @@ def tile_picked_hashbondquad_none_po_kernel(
     nc = tc.nc
     with ExitStack() as ctx:
         keep = ctx.enter_context(tc.tile_pool(name="keep", bufs=1))
-        psum = ctx.enter_context(tc.psum_pool(name="psum", bufs=8))
+        psum = ctx.enter_context(tc.psum_pool(name="psum", bufs=PSUM_BANKS))
 
         def sb(name, shape, dtype, tag=None):
             return keep.tile(shape, dtype, name=name, tag=tag or name, align_bytes=64)
@@ -65,23 +68,22 @@ def tile_picked_hashbondquad_none_po_kernel(
         nc.sync.dma_start(n3_t[:], n3)
         nc.sync.dma_start(n4_t[:], n4)
         nc.scalar.dma_start(out=ww_raw[:].bitcast(I32), in_=w1_words[0].bitcast(I32))
-        for q in range(4):
-            load_scale_rows(nc.scalar if q < 2 else nc.gpsimd, w1_scales, q)
+        for q in range(QUADS):
+            load_scale_rows(nc.scalar if q < QUADS // 2 else nc.gpsimd, w1_scales, q)
 
-        def deal_words(name, t0, t1, tag=None):
-            dealt = sb(name, [P, t1 - t0, 2 * P], U8, tag)
+        def deal_words(dealt, raw, t0):
             nc.vector.tensor_copy(
-                out=dealt[:].rearrange("p t (m b) -> p t m b", b=2),
-                in_=ww_raw[:].rearrange("p (m t b) -> p t m b", t=PACK, b=2)[:, t0:t1],
+                out=dealt.rearrange("p (t m b) -> p t m b", t=2, b=2),
+                in_=raw.rearrange("p (m t b) -> p t m b", t=PACK, b=2)[:, t0 : t0 + 2],
             )
-            return [dealt[:, t, :] for t in range(t1 - t0)]
+            return [dealt[:, 2 * P * t : 2 * P * (t + 1)] for t in range(2)]
 
-        def deal_scales(name, t0, t1, tag=None):
-            dealt = sb(name, [P, t1 - t0, P], U8, tag)
+        def deal_scales(dealt, t0):
             nc.vector.tensor_copy(
-                out=dealt[:], in_=ws_raw[:].rearrange("p (m t) -> p t m", t=PACK)[:, t0:t1]
+                out=dealt.rearrange("p (t m) -> p t m", t=2),
+                in_=ws_raw[:].rearrange("p (m t) -> p t m", t=PACK)[:, t0 : t0 + 2],
             )
-            return [dealt[:, t, :] for t in range(t1 - t0)]
+            return [dealt[:, P * t : P * (t + 1)] for t in range(2)]
 
         def product(ww, ws, t, words, scales, c0, c1):
             acc = psum.tile([P, c1 - c0], F32, name="acc")
@@ -98,23 +100,28 @@ def tile_picked_hashbondquad_none_po_kernel(
 
         xs_picked = sb("xs_picked", [P, S], U8)
         nc.vector.tensor_copy(out=xs_picked[:], in_=xs[:].indirect(offs_t[:]))
-        for q in range(4):
+        for q in range(QUADS):
             queue = nc.scalar if q % 2 == 0 else nc.sync
             queue.dma_start(
                 out=xs_placed[32 * q : 32 * q + 4, :].bitcast(I32),
                 in_=xs_picked[32 * q : 32 * q + 32 : 8, :].bitcast(I32),
             )
-        w1w = deal_words("w1w", 0, PACK, "xs")
-        nc.sync.dma_start(out=ww_raw[:].bitcast(I32), in_=w2_words[0].bitcast(I32))
+        after_xs = sb("after_xs", [P, 4 * P + 2 * N], U8, "xs")
+        w2w_raw = after_xs[:, 4 * P :]
+        nc.sync.dma_start(out=w2w_raw.bitcast(I32), in_=w2_words[0].bitcast(I32))
+        w1w = deal_words(after_xs[:, : 4 * P], ww_raw[:], 0)
         xw_picked = sb("xw_picked", [P, S], U32)
         for c0 in (0, HALF):
             nc.vector.tensor_copy(
                 out=xw_picked[:, c0 : c0 + HALF], in_=xw[:].bitcast(U32).indirect(entries(offs_t, c0, c0 + HALF))
             )
-        w1s = deal_scales("w1s", 0, PACK, "xw")
-        for q in range(4):
+        after_xw = sb("after_xw", [P, 8 * P], U8, "xw")
+        w1s = deal_scales(after_xw[:, : 2 * P], 0)
+        w1s = w1s + deal_scales(after_xw[:, 2 * P : 4 * P], 2)
+        w1w = w1w + deal_words(after_xw[:, 4 * P :], ww_raw[:], 2)
+        for q in range(QUADS):
             load_scale_rows(nc.sync, w2_scales, q)
-        w2w = deal_words("w2w_first", 0, 2, "xs_picked")
+        w2w = deal_words(sb("w2w_first", [P, 4 * P], U8, "xs_picked")[:], w2w_raw, 0)
 
         y = [sb(f"y{t}", [P, S], F32) for t in range(PACK)]
         for t in range(PACK):
@@ -168,7 +175,7 @@ def tile_picked_hashbondquad_none_po_kernel(
                 round_z_vector(t - 1, 0)
             put_product(t)
             if t == 0:
-                w2s = deal_scales("w2s_first", 0, 2, "y1")
+                w2s = deal_scales(sb("w2s_first", [P, 2 * P], U8, "y1")[:], 0)
             if t < 2:
                 round_z_scalar(t, 0)
             round_z_scalar(t, 1)
@@ -182,11 +189,11 @@ def tile_picked_hashbondquad_none_po_kernel(
                 out=zw[:, cols].bitcast(FP8X4), scales=zs[:, cols], in_=zb[h][:].rearrange("p c t -> p (c t)")
             )
 
-        hw = [sb(f"hw{t}", [P, 2 * S if t in (1, 2) else S], F32) for t in range(PACK)]
+        hw = [sb(f"hw{t}", [P, 2 * S if t == 1 else S], F32) for t in range(PACK)]
         hp = [sb(f"hp{t}", [P, S], F32) for t in range(PACK)]
         first = [product(w2w, w2s, 0, zw, zs, h * HALF, (h + 1) * HALF) for h in range(2)]
-        w2w = w2w + deal_words("w2w_rest", 2, PACK, "zb1")
-        w2s = w2s + deal_scales("w2s_rest", 2, PACK, "zb0")
+        w2w = w2w + deal_words(sb("w2w_rest", [P, 4 * P], U8, "zb1")[:], w2w_raw, 2)
+        w2s = w2s + deal_scales(sb("w2s_rest", [P, 2 * P], U8, "zb0")[:], 2)
         nc.scalar.copy(out=hw[0][:, :HALF], in_=first[0][:])
         nc.scalar.copy(out=hw[0][:, HALF:], in_=first[1][:])
         nc.vector.tensor_copy(out=hp[0][:, :HALF], in_=first[0][:])
@@ -198,12 +205,19 @@ def tile_picked_hashbondquad_none_po_kernel(
 
         d3 = sb("d3", [P, PACK, S], F32)
         d4 = sb("d4", [P, PACK, S], F32)
-        res = sb("res", [P, PACK, S], F32)
+        res01 = sb("res01", [P, 2, S], F32)
+        res23 = [sb(f"res23_{h}", [P, 2, HALF], F32) for h in range(2)]
         resb = sb("resb", [P, S, PACK], BF16)
         ow = sb("ow", [P, S], U32)
         osc = sb("osc", [P, S], U8)
         out_rows = out_0.rearrange("(p t) c -> p t c", t=PACK)
         out_words = out_1[0].rearrange("p c t -> p (c t)").bitcast(I32)
+
+        def res_pair(t, c0, c1):
+            if t < 2:
+                return res01[:, :, c0:c1]
+            h = c0 // HALF
+            return res23[h][:, :, c0 - h * HALF : c1 - h * HALF]
 
         def diff(dst, lst, t, c0, c1):
             nc.vector.tensor_tensor(
@@ -211,13 +225,14 @@ def tile_picked_hashbondquad_none_po_kernel(
             )
 
         def finish(t, c0, c1):
+            res = res_pair(t, c0, c1)[:, t % 2, :]
             nc.vector.scalar_tensor_tensor(
-                out=res[:, t, c0:c1], in0=d3[:, t, c0:c1], scalar=0.75, in1=d4[:, t, c0:c1], op0=ALU.mult, op1=ALU.mult
+                out=res, in0=d3[:, t, c0:c1], scalar=0.75, in1=d4[:, t, c0:c1], op0=ALU.mult, op1=ALU.mult
             )
-            nc.sync.dma_start(out=out_rows[:, t, c0:c1], in_=res[:, t, c0:c1])
+            nc.sync.dma_start(out=out_rows[:, t, c0:c1], in_=res)
 
-        def round_out(copy, t0, c0, c1):
-            copy(out=resb[:, c0:c1, t0 : t0 + 2], in_=res[:, t0 : t0 + 2, c0:c1].rearrange("p t c -> p c t"))
+        def round_pair(copy, t, c0, c1):
+            copy(out=resb[:, c0:c1, t - 1 : t + 1], in_=res_pair(t, c0, c1).rearrange("p t c -> p c t"))
 
         def quantise_out(c0, c1):
             nc.vector.quantize_mx(
@@ -227,34 +242,22 @@ def tile_picked_hashbondquad_none_po_kernel(
             )
             nc.sync.dma_start(out=out_words[:, c0:c1], in_=ow[:, c0:c1].bitcast(I32))
 
-        diff(d3, n3_t, 0, 0, HALF)
-        diff(d4, n4_t, 0, 0, HALF)
-        diff(d3, n3_t, 0, HALF, S)
-        diff(d4, n4_t, 0, HALF, S)
-        for t in (1, 2):
-            diff(d3, n3_t, t, 0, S)
-            finish(t - 1, 0, S)
-            diff(d4, n4_t, t, 0, S)
-        round_out(nc.scalar.copy, 0, 0, S)
-        t = PACK - 1
-        a, b = HALF, HALF + HALF // 2
-        diff(d3, n3_t, t, 0, a)
-        finish(t - 1, 0, S)
-        diff(d4, n4_t, t, 0, a)
-        diff(d3, n3_t, t, a, b)
-        finish(t, 0, a)
-        round_out(nc.scalar.copy, 2, 0, a)
-        diff(d4, n4_t, t, a, b)
-        diff(d3, n3_t, t, b, S)
-        finish(t, a, b)
-        round_out(nc.scalar.copy, 2, a, b)
-        diff(d4, n4_t, t, b, S)
-        quantise_out(0, a)
-        finish(t, b, S)
-        quantise_out(a, b)
-        round_out(nc.vector.tensor_copy, 2, b, S)
-        quantise_out(b, S)
-        for q in range(4):
+        for c0 in (0, HALF):
+            diff(d3, n3_t, 0, c0, c0 + HALF)
+            diff(d4, n4_t, 0, c0, c0 + HALF)
+        pieces = [(0, 0, S), (1, 0, S), (2, 0, HALF), (3, 0, HALF), (2, HALF, S), (3, HALF, LAST), (3, LAST, S)]
+        for before, piece in zip(pieces, pieces[1:]):
+            diff(d3, n3_t, *piece)
+            finish(*before)
+            if before[0] % 2 == 1:
+                round_pair(nc.scalar.copy, *before)
+            diff(d4, n4_t, *piece)
+        quantise_out(0, HALF)
+        finish(*pieces[-1])
+        quantise_out(HALF, LAST)
+        round_pair(nc.vector.tensor_copy, *pieces[-1])
+        quantise_out(LAST, S)
+        for q in range(QUADS):
             queue = nc.scalar if q % 2 == 0 else nc.sync
             queue.dma_start(
                 out=out_2[0][4 * q : 4 * q + 4, :].bitcast(I32), in_=osc[32 * q : 32 * q + 4, :].bitcast(I32)

from contextlib import ExitStack

import concourse.mybir as mybir

K, T, S, N, H, W = 512, 2048, 512, 512, 512, 256
FLOPS = 2 * K * H * S + 2 * H * N * S

F32 = mybir.dt.float32
BF16 = mybir.dt.bfloat16
I32 = mybir.dt.int32
U32 = mybir.dt.uint32
U16 = mybir.dt.uint16
U8 = mybir.dt.uint8
FP8X4 = mybir.dt.float8_e4m3fn_x4
FP4X4 = mybir.dt.float4_e2m1fn_x4
ALU = mybir.AluOpType
COPY = mybir.ActivationFunctionType.Copy

P = 128
PACK = 4
QUADS = 4
HALF = S // 2
LAST = S - S // 4
PER_COL = 16
PSUM_BANKS = 8


def tile_picked_hashbondquad_none_po_kernel(
    tc, x_words, x_scales, w1_words, w1_scales, gn, w2_words, w2_scales, offs, n1, n2, n3, n4, out_0, out_1, out_2
):
    nc = tc.nc
    with ExitStack() as ctx:
        keep = ctx.enter_context(tc.tile_pool(name="keep", bufs=1))
        psum = ctx.enter_context(tc.psum_pool(name="psum", bufs=PSUM_BANKS))

        def sb(name, shape, dtype, tag=None):
            return keep.tile(shape, dtype, name=name, tag=tag or name, align_bytes=64)

        def entries(lst, c0, c1):
            return lst[:, c0 // PER_COL : c1 // PER_COL]

        offs_t = keep.tile([P, S // PER_COL], U16, name="offs_t")
        n1_t = keep.tile([P, W // PER_COL], U16, name="n1_t")
        n2_t = keep.tile([P, W // PER_COL], U16, name="n2_t")
        n3_t = keep.tile([P, S // PER_COL], U16, name="n3_t")
        n4_t = keep.tile([P, S // PER_COL], U16, name="n4_t")

        xw = sb("xw", [P, T], I32)
        xs = sb("xs", [P, T], U8)
        ww_raw = sb("ww_raw", [P, 2 * H], U8)
        ws_raw = sb("ws_raw", [P, H], U8)
        xs_placed = sb("xs_placed", [P, S], U8)

        nc.gpsimd.memset(xs[:].bitcast(I32), 0)
        nc.vector.memset(ws_raw[:].bitcast(I32), 0)
        nc.vector.memset(xs_placed[:].bitcast(I32), 0)

        def load_scale_rows(queue, scales, q):
            queue.dma_start(
                out=ws_raw[32 * q : 32 * q + 4, :].bitcast(I32), in_=scales[0][4 * q : 4 * q + 4, :].bitcast(I32)
            )

        nc.sync.dma_start(offs_t[:], offs)
        nc.sync.dma_start(out=xs[0:P:8, :].bitcast(I32), in_=x_scales[0].bitcast(I32))
        nc.sync.dma_start(n1_t[:], n1)
        nc.sync.dma_start(out=xw[:], in_=x_words[0].rearrange("p n t -> p (n t)").bitcast(I32))
        nc.sync.dma_start(n2_t[:], n2)
        nc.sync.dma_start(n3_t[:], n3)
        nc.sync.dma_start(n4_t[:], n4)
        nc.scalar.dma_start(out=ww_raw[:].bitcast(I32), in_=w1_words[0].bitcast(I32))
        for q in range(QUADS):
            load_scale_rows(nc.scalar if q < QUADS // 2 else nc.gpsimd, w1_scales, q)

        def deal_words(dealt, raw, t0):
            nc.vector.tensor_copy(
                out=dealt.rearrange("p (t m b) -> p t m b", t=2, b=2),
                in_=raw.rearrange("p (m t b) -> p t m b", t=PACK, b=2)[:, t0 : t0 + 2],
            )
            return [dealt[:, 2 * P * t : 2 * P * (t + 1)] for t in range(2)]

        def deal_scales(dealt, t0):
            nc.vector.tensor_copy(
                out=dealt.rearrange("p (t m) -> p t m", t=2),
                in_=ws_raw[:].rearrange("p (m t) -> p t m", t=PACK)[:, t0 : t0 + 2],
            )
            return [dealt[:, P * t : P * (t + 1)] for t in range(2)]

        def product(ww, ws, t, words, scales, c0, c1):
            acc = psum.tile([P, c1 - c0], F32, name="acc")
            nc.tensor.matmul_mx(
                out=acc[:],
                lhsT=ww[t].bitcast(FP4X4),
                lhsT_scale=ws[t],
                rhs=words[:, c0:c1].bitcast(FP8X4),
                rhs_scale=scales[:, c0:c1],
                start=True,
                stop=True,
            )
            return acc

        xs_picked = sb("xs_picked", [P, S], U8)
        nc.vector.tensor_copy(out=xs_picked[:], in_=xs[:].indirect(offs_t[:]))
        for q in range(QUADS):
            queue = nc.scalar if q % 2 == 0 else nc.sync
            queue.dma_start(
                out=xs_placed[32 * q : 32 * q + 4, :].bitcast(I32),
                in_=xs_picked[32 * q : 32 * q + 32 : 8, :].bitcast(I32),
            )
        after_xs = sb("after_xs", [P, 4 * P + 2 * N], U8, "xs")
        w2w_raw = after_xs[:, 4 * P :]
        nc.sync.dma_start(out=w2w_raw.bitcast(I32), in_=w2_words[0].bitcast(I32))
        w1w = deal_words(after_xs[:, : 4 * P], ww_raw[:], 0)
        xw_picked = sb("xw_picked", [P, S], U32)
        for c0 in (0, HALF):
            nc.vector.tensor_copy(
                out=xw_picked[:, c0 : c0 + HALF], in_=xw[:].bitcast(U32).indirect(entries(offs_t, c0, c0 + HALF))
            )
        after_xw = sb("after_xw", [P, 8 * P], U8, "xw")
        w1s = deal_scales(after_xw[:, : 2 * P], 0)
        w1s = w1s + deal_scales(after_xw[:, 2 * P : 4 * P], 2)
        w1w = w1w + deal_words(after_xw[:, 4 * P :], ww_raw[:], 2)
        for q in range(QUADS):
            load_scale_rows(nc.sync, w2_scales, q)
        w2w = deal_words(sb("w2w_first", [P, 4 * P], U8, "xs_picked")[:], w2w_raw, 0)

        y = [sb(f"y{t}", [P, S], F32) for t in range(PACK)]
        for t in range(PACK):
            for c0, c1 in ((0, HALF), (HALF, S)) if t == 0 else ((0, S),):
                acc = product(w1w, w1s, t, xw_picked, xs_placed, c0, c1)
                nc.scalar.copy(out=y[t][:, c0:c1], in_=acc[:])

        gain = sb("gain", [P, PACK], F32, "xw_picked")
        nc.sync.dma_start(out=gain[:], in_=gn.rearrange("(p t) o -> p (t o)", t=PACK))
        pa = [sb(f"pa{t}", [P, W], F32) for t in range(PACK)]
        pb = [sb(f"pb{t}", [P, W], F32) for t in range(PACK)]
        dt = [sb(f"dt{t}", [P, S], F32) for t in range(PACK)]
        zb = [sb(f"zb{h}", [P, HALF, PACK], BF16) for h in range(2)]

        def fetch_a(t):
            nc.vector.tensor_copy(out=pa[t][:], in_=y[t][:].indirect(n1_t[:]))

        def fetch_b(t):
            nc.vector.tensor_copy(out=pb[t][:], in_=y[t][:].indirect(n2_t[:]))

        def put_sum(t):
            nc.vector.tensor_tensor(dt[t][:].indirect(n1_t[:]), pa[t][:], pb[t][:], ALU.add)

        def put_product(t):
            nc.vector.tensor_tensor(dt[t][:].indirect(n2_t[:]), pa[t][:], pb[t][:], ALU.mult)

        def round_z_scalar(t, h):
            nc.scalar.activation(
                out=zb[h][:, :, t], in_=dt[t][:, h * HALF : (h + 1) * HALF], func=COPY, scale=gain[:, t : t + 1]
            )

        def round_z_vector(t, h):
            nc.vector.tensor_scalar(
                out=zb[h][:, :, t],
                in0=dt[t][:, h * HALF : (h + 1) * HALF],
                scalar1=gain[:, t : t + 1],
                scalar2=None,
                op0=ALU.mult,
            )

        fetch_a(0)
        fetch_b(0)
        for t in range(PACK):
            last = t == PACK - 1
            if not last:
                fetch_a(t + 1)
            put_sum(t)
            if not last:
                fetch_b(t + 1)
            else:
                round_z_vector(t - 1, 0)
            put_product(t)
            if t == 0:
                w2s = deal_scales(sb("w2s_first", [P, 2 * P], U8, "y1")[:], 0)
            if t < 2:
                round_z_scalar(t, 0)
            round_z_scalar(t, 1)
        round_z_vector(PACK - 1, 0)

        zw = sb("zw", [P, S], U32)
        zs = sb("zs", [P, S], U8)
        for h in range(2):
            cols = slice(h * HALF, (h + 1) * HALF)
            nc.vector.quantize_mx(
                out=zw[:, cols].bitcast(FP8X4), scales=zs[:, cols], in_=zb[h][:].rearrange("p c t -> p (c t)")
            )

        hw = [sb(f"hw{t}", [P, 2 * S if t == 1 else S], F32) for t in range(PACK)]
        hp = [sb(f"hp{t}", [P, S], F32) for t in range(PACK)]
        first = [product(w2w, w2s, 0, zw, zs, h * HALF, (h + 1) * HALF) for h in range(2)]
        w2w = w2w + deal_words(sb("w2w_rest", [P, 4 * P], U8, "zb1")[:], w2w_raw, 2)
        w2s = w2s + deal_scales(sb("w2s_rest", [P, 2 * P], U8, "zb0")[:], 2)
        nc.scalar.copy(out=hw[0][:, :HALF], in_=first[0][:])
        nc.scalar.copy(out=hw[0][:, HALF:], in_=first[1][:])
        nc.vector.tensor_copy(out=hp[0][:, :HALF], in_=first[0][:])
        nc.scalar.copy(out=hp[0][:, HALF:], in_=first[1][:])
        for t in range(1, PACK):
            acc = product(w2w, w2s, t, zw, zs, 0, S)
            nc.scalar.copy(out=hw[t][:, :S], in_=acc[:])
            nc.scalar.copy(out=hp[t][:], in_=acc[:])

        d3 = sb("d3", [P, PACK, S], F32)
        d4 = sb("d4", [P, PACK, S], F32)
        res01 = sb("res01", [P, 2, S], F32)
        res23 = [sb(f"res23_{h}", [P, 2, HALF], F32) for h in range(2)]
        resb = sb("resb", [P, S, PACK], BF16)
        ow = sb("ow", [P, S], U32)
        osc = sb("osc", [P, S], U8)
        out_rows = out_0.rearrange("(p t) c -> p t c", t=PACK)
        out_words = out_1[0].rearrange("p c t -> p (c t)").bitcast(I32)

        def res_pair(t, c0, c1):
            if t < 2:
                return res01[:, :, c0:c1]
            h = c0 // HALF
            return res23[h][:, :, c0 - h * HALF : c1 - h * HALF]

        def diff(dst, lst, t, c0, c1):
            nc.vector.tensor_tensor(
                dst[:, t, c0:c1], hw[t][:].indirect(entries(lst, c0, c1)), hp[t][:, c0:c1], ALU.subtract
            )

        def finish(t, c0, c1):
            res = res_pair(t, c0, c1)[:, t % 2, :]
            nc.vector.scalar_tensor_tensor(
                out=res, in0=d3[:, t, c0:c1], scalar=0.75, in1=d4[:, t, c0:c1], op0=ALU.mult, op1=ALU.mult
            )
            nc.sync.dma_start(out=out_rows[:, t, c0:c1], in_=res)

        def round_pair(copy, t, c0, c1):
            copy(out=resb[:, c0:c1, t - 1 : t + 1], in_=res_pair(t, c0, c1).rearrange("p t c -> p c t"))

        def quantise_out(c0, c1):
            nc.vector.quantize_mx(
                out=ow[:, c0:c1].bitcast(FP8X4),
                scales=osc[:, c0:c1],
                in_=resb[:, c0:c1, :].rearrange("p c t -> p (c t)"),
            )
            nc.sync.dma_start(out=out_words[:, c0:c1], in_=ow[:, c0:c1].bitcast(I32))

        for c0 in (0, HALF):
            diff(d3, n3_t, 0, c0, c0 + HALF)
            diff(d4, n4_t, 0, c0, c0 + HALF)
        pieces = [(0, 0, S), (1, 0, S), (2, 0, HALF), (3, 0, HALF), (2, HALF, S), (3, HALF, LAST), (3, LAST, S)]
        for before, piece in zip(pieces, pieces[1:]):
            diff(d3, n3_t, *piece)
            finish(*before)
            if before[0] % 2 == 1:
                round_pair(nc.scalar.copy, *before)
            diff(d4, n4_t, *piece)
        quantise_out(0, HALF)
        finish(*pieces[-1])
        quantise_out(HALF, LAST)
        round_pair(nc.vector.tensor_copy, *pieces[-1])
        quantise_out(LAST, S)
        for q in range(QUADS):
            queue = nc.scalar if q % 2 == 0 else nc.sync
            queue.dma_start(
                out=out_2[0][4 * q : 4 * q + 4, :].bitcast(I32), in_=osc[32 * q : 32 * q + 4, :].bitcast(I32)
            )
